import numpy as np
import ml_dtypes


def mxq(x, axis, fmt="e4m3"):
    dtype, down = {"e4m3": (ml_dtypes.float8_e4m3fn, 7), "e5m2": (ml_dtypes.float8_e5m2, 14)}[fmt]
    v = np.moveaxis(np.asarray(x, np.float32).astype(ml_dtypes.bfloat16).astype(np.float64), axis, -1)
    blocks = v.reshape(v.shape[:-1] + (-1, 32))
    amax = np.abs(blocks).max(-1, keepdims=True)
    byte = np.maximum(np.where(amax > 0, np.frexp(amax)[1] - 1 + 127, 0) - down, 1)
    scale = np.exp2(byte - 127.0)
    codes = (blocks / scale).astype(np.float32).astype(dtype).astype(np.float64)
    return np.moveaxis((codes * scale).reshape(v.shape), -1, axis)


WIDE = False


def mx_kscale(k):
    if not WIDE:
        return np.ones(k)
    levels = np.array([10, -10, 5, -5, 0])
    if k % 512:
        return np.exp2(np.random.permutation(np.resize(levels, k // 32))).repeat(32)
    a = np.empty((k // 512, 16))
    for p in range(k // 512):
        a[p, :8] = np.random.permutation(np.resize(levels, 8))
        for g in range(8):
            far = levels[np.abs(levels - a[p, g]) >= 10]
            a[p, g + 8] = far[np.random.randint(len(far))]
    return np.exp2(a.ravel()).repeat(32)


def f64(x):
    return np.asarray(x).astype(np.float64)


def striped(idx):
    return np.tile(idx.reshape(-1, 16).T, (8, 1)).astype(np.uint16)


def unstriped(offs):
    return offs[:16].T.reshape(-1).astype(np.int64)


E2M1 = np.array([0.0, 0.5, 1.0, 1.5, 2.0, 3.0, 4.0, 6.0, -0.0, -0.5, -1.0, -1.5, -2.0, -3.0, -4.0, -6.0])


def pack_fp4(w):
    k, n = w.shape
    w = f64(np.asarray(w, np.float32).astype(ml_dtypes.bfloat16)).reshape(k // 32, 32, n)
    amax = np.abs(w).max(1)
    mant, ex = np.frexp(amax / 6.0)
    byte = np.clip(np.where(amax > 0, np.where(mant > 0.5, ex, ex - 1) + 127, 1), 1, 254)
    scaled = (w * np.exp2(127.0 - byte)[:, None, :]).reshape(k, n).astype(np.float32)
    c = np.ascontiguousarray(scaled.reshape(k // 512, 128, 4, n).transpose(0, 1, 3, 2)).astype(ml_dtypes.float4_e2m1fn).view(np.uint8) & 0xF
    words = (c[..., 0::2] | (c[..., 1::2] << 4)).reshape(k // 512, 128, 2 * n)
    return np.ascontiguousarray(words), np.ascontiguousarray(byte.astype(np.uint8).reshape(k // 512, 16, n))


def unpack_fp4(words, scales):
    g, _, n = scales.shape
    words = np.ascontiguousarray(words).reshape(g, 128, n, 2)
    nib = np.empty((g, 128, n, 4), np.uint8)
    nib[..., 0::2] = words & 0xF
    nib[..., 1::2] = words >> 4
    vals = E2M1[nib] * np.repeat(np.exp2(scales.astype(np.float64) - 127.0), 8, axis=1)[..., None]
    return vals.transpose(0, 1, 3, 2).reshape(g * 512, n)


def relu(v):
    return np.maximum(v, 0.0)


K, T, D, N = 512, 512, 4, 256
P = 2 ** 7


def setup_inputs():
    n = np.random.standard_normal
    s = mx_kscale(K)[:, None]
    packed_xT = pack_fp4(n((K, T)) * s)
    return {
        "x_words": packed_xT[0],
        "x_scales": packed_xT[1],
        "w1": (n((K, N)) / np.sqrt(K) / s).astype(np.float32),
        "score": np.tile(np.random.standard_normal((D, 1, T)), (1, P, 1)).astype(np.float32),
        "pos1": striped(np.random.permutation(T)),
        "pos2": striped(np.random.permutation(T)),
        "pos3": striped(np.random.permutation(T)),
        "pos4": striped(np.random.permutation(T)),
    }


def reference(x_words, x_scales, w1, score, pos1, pos2, pos3, pos4):
    xq = unpack_fp4(x_words, x_scales)
    y = mxq(f64(w1), 0, "e4m3").T @ xq
    e0 = np.exp(f64(score)[0, :1])
    e1 = np.exp(f64(score)[1, :1])
    e2 = np.exp(f64(score)[2, :1])
    e3 = np.exp(f64(score)[3, :1])
    num = y[:, unstriped(pos1)] * e0 + y[:, unstriped(pos2)] * e1 + y[:, unstriped(pos3)] * e2 + y[:, unstriped(pos4)] * e3
    den = e0 + e1 + e2 + e3
    return relu(num / den)

@@ -1,0 +1,201 @@
+from contextlib import ExitStack
+
+import concourse.mybir as mybir
+
+K, T, D, N = 512, 512, 4, 256
+P = 128
+PACK = 4
+PAD = 192
+
+FLOPS = 2 * K * N * T
+BYTES = K * T // 2 + K * T // 32 + 4 * K * N + 4 * D * T + 2 * D * P * (T // 16) + 4 * N * T
+
+F32 = mybir.dt.float32
+BF16 = mybir.dt.bfloat16
+I32 = mybir.dt.int32
+U32 = mybir.dt.uint32
+U16 = mybir.dt.uint16
+U8 = mybir.dt.uint8
+FP8X4 = mybir.dt.float8_e4m3fn_x4
+FP4X4 = mybir.dt.float4_e2m1fn_x4
+ALU = mybir.AluOpType
+ACT = mybir.ActivationFunctionType
+AX = mybir.AxisListType
+
+
+def tile_picked_wgatv_relu_l_kernel(
+    tc, x_words, x_scales, w1, score, pos1, pos2, pos3, pos4, out
+):
+    nc = tc.nc
+    with ExitStack() as ctx:
+        keep = ctx.enter_context(tc.tile_pool(name="keep", bufs=1))
+        psum = ctx.enter_context(tc.psum_pool(name="psum", bufs=1))
+
+        def bank(k, shape, name):
+            return psum.tile(shape, F32, tag="bank%d" % k, name=name)
+
+        w_raw = [keep.tile([P, PACK, P], F32, name="w_raw%d" % b) for b in range(2)]
+        w_rows = w1.rearrange("(p j) n -> p j n", j=PACK)
+        nc.sync.dma_start(w_raw[0][:], w_rows[:, :, 0:P])
+        s_rows = keep.tile([P, P], F32, name="s_rows")
+        nc.sync.dma_start(s_rows[:], score.rearrange("d r (c q) -> (r c) d q", q=P)[0:32])
+        xw = keep.tile([P, 2 * T], U8, name="xw", align_bytes=64)
+        nc.sync.dma_start(xw[:].bitcast(I32), x_words[0].bitcast(I32))
+        xs = keep.tile([P, T], U8, name="xs", align_bytes=64)
+        for q in range(4):
+            nc.scalar.dma_start(
+                xs[32 * q : 32 * (q + 1), :].bitcast(I32),
+                x_scales[0, 4 * q : 4 * (q + 1), :].bitcast(I32).partition_broadcast(8),
+            )
+        lists = []
+        for d, pos in enumerate((pos1, pos2, pos3, pos4)):
+            offsets = keep.tile([P, T // 16], U16, name="offsets%d" % d)
+            nc.sync.dma_start(offsets[:], pos)
+            lists.append(offsets)
+            if d == 1:
+                nc.sync.dma_start(w_raw[1][:], w_rows[:, :, P : 2 * P])
+
+        ident = keep.tile([P, P], F32, name="ident")
+        ones = keep.tile([P, 32], F32, name="ones")
+        nc.vector.memset(ones[:], 1.0)
+        nc.gpsimd.memset(ident[:], 0.0)
+        column = keep.tile([P, 32], F32, name="column", align_bytes=64)
+        nc.vector.tensor_tensor_scan(column[:], ones[:], ones[:], 0.0, ALU.mult, ALU.add)
+        row = keep.tile([P, 32], F32, name="row", align_bytes=64)
+        nc.vector.transpose(row[:], column[:])
+        for q in range(4):
+            part = slice(32 * q, 32 * (q + 1))
+            nc.vector.tensor_tensor(ident[part, part], column[part, :], row[part, :], ALU.is_equal)
+        y = []
+        for b in range(2):
+            yb = keep.tile([P, T + PAD], F32, name="y%d" % b)
+            nc.gpsimd.memset(yb[:, T:], 0.0)
+            y.append(yb)
+
+        s_ps = bank(0, [P, P], "s_ps")
+        nc.tensor.transpose(s_ps[:], s_rows[:], ident[:])
+        s = s_ps[:, 0:16].rearrange("q (c d) -> q c d", d=D)
+        top = keep.tile([P, 4], F32, name="top")
+        nc.vector.tensor_reduce(top[:], s, AX.X, ALU.max)
+        shifted = keep.tile([P, 4, D], F32, name="shifted")
+        nc.vector.tensor_tensor(shifted[:], s, top[:].unsqueeze(2).to_broadcast([P, 4, D]), ALU.subtract)
+        e = keep.tile([P, 4, D], F32, name="e")
+        nc.scalar.activation(e[:], shifted[:], ACT.Exp)
+        den = keep.tile([P, 4], F32, name="den")
+        nc.vector.tensor_reduce(den[:], e[:], AX.X, ALU.add)
+        inv = keep.tile([P, 4], F32, name="inv")
+        nc.vector.reciprocal(inv[:], den[:])
+        a0 = keep.tile([P, 4], F32, name="a0")
+        nc.vector.tensor_tensor(a0[:], e[:, :, 0], inv[:], ALU.mult)
+
+        def quantise(b, engine_copy):
+            grouped = keep.tile([P, P, PACK], BF16, name="grouped%d" % b, align_bytes=64)
+            engine_copy(
+                grouped[:].rearrange("p (c i) t -> p c t i", i=4),
+                w_raw[b][:].rearrange("p t (c i) -> p c t i", i=4),
+            )
+            codes = keep.tile([P, P], U32, name="codes%d" % b, align_bytes=64)
+            scales = keep.tile([P, P], U8, name="scales%d" % b, align_bytes=64)
+            nc.vector.quantize_mx(codes[:].bitcast(FP8X4), scales[:], grouped[:].rearrange("p m t -> p (m t)"))
+            return codes, scales
+
+        def project(b, w_mx, k, c0, c1, engine_copy):
+            codes, scales = w_mx
+            acc = bank(k, [P, c1 - c0], "acc%d_%d" % (b, c0))
+            nc.tensor.matmul_mx(
+                acc[:], lhsT=codes[:].bitcast(FP8X4), lhsT_scale=scales[:],
+                rhs=xw[:, 2 * c0 : 2 * c1].bitcast(FP4X4), rhs_scale=xs[:, c0:c1], start=True, stop=True,
+            )
+            engine_copy(y[b][:, c0:c1], acc[:])
+
+        def spread(d, k):
+            ps = bank(k, [P, 4, P], "spread%d" % d)
+            for c in range(4):
+                nc.tensor.transpose(ps[:, c, :], shifted[:, c, d : d + 1].to_broadcast([P, P]), ident[:])
+            wide = keep.tile([P, T], F32, name="wide%d" % d)
+            nc.scalar.activation(wide[:], ps[:].rearrange("p c n -> p (c n)"), ACT.Exp)
+            return wide
+
+        w0 = quantise(0, nc.vector.tensor_copy)
+        project(0, w0, 1, 0, T // 2, nc.vector.tensor_copy)
+        project(0, w0, 2, T // 2, T, nc.scalar.copy)
+        wide = {}
+        wide[1] = spread(1, 1)
+        w1q = quantise(1, nc.scalar.copy)
+        wide[2] = spread(2, 2)
+        wide[3] = spread(3, 1)
+        project(1, w1q, 3, 0, T, nc.scalar.copy)
+        wide[0] = spread(0, 2)
+
+        def gather(b, d, h, c0, c1):
+            nc.vector.tensor_tensor(
+                h[:, c0:c1], y[b][:].indirect(lists[d][:, c0 // 16 : c1 // 16]), wide[d][:, c0:c1], ALU.mult
+            )
+
+        def add_turned(h, acc, d, c0, c1, first=0):
+            n = (c1 - c0) // P
+            for c in range(n):
+                nc.tensor.matmul(
+                    acc[:, c, :], lhsT=h[:, c0 + c * P : c0 + (c + 1) * P], rhs=ident[:], is_transpose=True,
+                    start=(d == first and c == 0), stop=(d == D - 1 and c == n - 1),
+                )
+
+        def finish(b, acc, k, c0, c1, on_vector):
+            n = (c1 - c0) // P
+            turned = keep.tile([P, n, P], F32, name="turned%d_%d" % (b, c0))
+            for c in range(n):
+                scale = inv[:, c0 // P + c : c0 // P + c + 1]
+                if on_vector:
+                    nc.vector.tensor_scalar(turned[:, c, :], acc[:, c, :], scale, 0.0, ALU.mult, ALU.max)
+                else:
+                    nc.scalar.activation(turned[:, c, :], acc[:, c, :], ACT.Relu, scale=scale)
+            back = bank(k, [P, n, P], "back%d_%d" % (b, c0))
+            for c in range(n):
+                nc.tensor.transpose(back[:, c, :], turned[:, c, :], ident[:])
+            res = keep.tile([P, n, P], F32, name="res%d_%d" % (b, c0))
+            if on_vector:
+                nc.vector.tensor_copy(res[:], back[:])
+            else:
+                nc.scalar.copy(res[:], back[:])
+            nc.sync.dma_start(out[b * P : (b + 1) * P, c0:c1], res[:].rearrange("p c n -> p (c n)"))
+
+        g = keep.tile([P, T], F32, name="g0")
+        nc.vector.tensor_copy(g[:], y[0][:].indirect(lists[0][:]))
+        g_ps = bank(4, [P, 4, P], "g_ps")
+        for c in range(4):
+            nc.tensor.transpose(g_ps[:, c, :], g[:, c * P : (c + 1) * P], ident[:])
+        g_turned = keep.tile([P, 4, P], F32, name="g_turned")
+        for c in range(4):
+            nc.scalar.activation(g_turned[:, c, :], g_ps[:, c, :], ACT.Copy, scale=a0[:, c : c + 1])
+        acc0 = bank(5, [P, 4, P], "sum0")
+        for d in range(1, D):
+            h = keep.tile([P, T], F32, name="h0_%d" % d)
+            gather(0, d, h, 0, T)
+            add_turned(h, acc0, d, 0, T, 1)
+        turned0 = keep.tile([P, 4, P], F32, name="turned0")
+        for c in range(4):
+            nc.scalar.activation(turned0[:, c, :], acc0[:, c, :], ACT.Copy, scale=inv[:, c : c + 1])
+        back0 = bank(0, [P, 4, P], "back0")
+        for j, src in enumerate((g_turned, turned0)):
+            for c in range(4):
+                nc.tensor.matmul(
+                    back0[:, c, :], lhsT=src[:, c, :], rhs=ident[:], is_transpose=True,
+                    start=(j == 0 and c == 0), stop=(j == 1 and c == 3),
+                )
+        res0 = keep.tile([P, T], F32, name="res0")
+        nc.scalar.activation(res0[:], back0[:].rearrange("p c n -> p (c n)"), ACT.Relu)
+        nc.sync.dma_start(out[0:P, :], res0[:])
+
+        pieces = ((0, 256, 4, 1), (256, 384, 6, 2), (384, 512, 7, 3))
+        accs = [bank(k, [P, (c1 - c0) // P, P], "sum1_%d" % c0) for c0, c1, k, kb in pieces]
+        for d in range(D - 1):
+            h = keep.tile([P, T], F32, name="h1_%d" % d)
+            gather(1, d, h, 0, T)
+            for acc, (c0, c1, k, kb) in zip(accs, pieces):
+                add_turned(h, acc, d, c0, c1)
+        h = keep.tile([P, T], F32, name="h1_3")
+        for acc, (c0, c1, k, kb) in zip(accs, pieces):
+            gather(1, D - 1, h, c0, c1)
+            add_turned(h, acc, D - 1, c0, c1)
+        for acc, (c0, c1, k, kb) in zip(accs, pieces):
+            finish(1, acc, kb, c0, c1, c1 == T)

@@ -41,6 +41,7 @@ def tile_picked_wgatv_relu_l_kernel(
         nc.sync.dma_start(s_rows[:], score.rearrange("d r (c q) -> (r c) d q", q=P)[0:32])
         xw = keep.tile([P, 2 * T], U8, name="xw", align_bytes=64)
         nc.sync.dma_start(xw[:].bitcast(I32), x_words[0].bitcast(I32))
+        nc.sync.dma_start(w_raw[1][:], w_rows[:, :, P : 2 * P])
         xs = keep.tile([P, T], U8, name="xs", align_bytes=64)
         for q in range(4):
             nc.scalar.dma_start(
@@ -52,8 +53,6 @@ def tile_picked_wgatv_relu_l_kernel(
             offsets = keep.tile([P, T // 16], U16, name="offsets%d" % d)
             nc.sync.dma_start(offsets[:], pos)
             lists.append(offsets)
-            if d == 1:
-                nc.sync.dma_start(w_raw[1][:], w_rows[:, :, P : 2 * P])
 
         ident = keep.tile([P, P], F32, name="ident")
         ones = keep.tile([P, 32], F32, name="ones")
@@ -72,32 +71,35 @@ def tile_picked_wgatv_relu_l_kernel(
             nc.gpsimd.memset(yb[:, T:], 0.0)
             y.append(yb)
 
-        s_ps = bank(0, [P, P], "s_ps")
-        nc.tensor.transpose(s_ps[:], s_rows[:], ident[:])
-        s = s_ps[:, 0:16].rearrange("q (c d) -> q c d", d=D)
-        top = keep.tile([P, 4], F32, name="top")
-        nc.vector.tensor_reduce(top[:], s, AX.X, ALU.max)
-        shifted = keep.tile([P, 4, D], F32, name="shifted")
-        nc.vector.tensor_tensor(shifted[:], s, top[:].unsqueeze(2).to_broadcast([P, 4, D]), ALU.subtract)
-        e = keep.tile([P, 4, D], F32, name="e")
-        nc.scalar.activation(e[:], shifted[:], ACT.Exp)
-        den = keep.tile([P, 4], F32, name="den")
-        nc.vector.tensor_reduce(den[:], e[:], AX.X, ALU.add)
-        inv = keep.tile([P, 4], F32, name="inv")
-        nc.vector.reciprocal(inv[:], den[:])
-        a0 = keep.tile([P, 4], F32, name="a0")
-        nc.vector.tensor_tensor(a0[:], e[:, :, 0], inv[:], ALU.mult)
-
-        def quantise(b, engine_copy):
+        def quantise(b, copies):
             grouped = keep.tile([P, P, PACK], BF16, name="grouped%d" % b, align_bytes=64)
-            engine_copy(
-                grouped[:].rearrange("p (c i) t -> p c t i", i=4),
-                w_raw[b][:].rearrange("p t (c i) -> p c t i", i=4),
-            )
+            n = P // len(copies)
+            for j, engine_copy in enumerate(copies):
+                engine_copy(
+                    grouped[:, j * n : (j + 1) * n, :].rearrange("p (c i) t -> p c t i", i=4),
+                    w_raw[b][:, :, j * n : (j + 1) * n].rearrange("p t (c i) -> p c t i", i=4),
+                )
             codes = keep.tile([P, P], U32, name="codes%d" % b, align_bytes=64)
             scales = keep.tile([P, P], U8, name="scales%d" % b, align_bytes=64)
             nc.vector.quantize_mx(codes[:].bitcast(FP8X4), scales[:], grouped[:].rearrange("p m t -> p (m t)"))
             return codes, scales
+
+        w0 = quantise(0, (nc.vector.tensor_copy,))
+        s_ps = bank(0, [P, P], "s_ps")
+        nc.tensor.transpose(s_ps[:], s_rows[:], ident[:])
+        s = s_ps[:, 0:16].rearrange("q (c d) -> q c d", d=D)
+        minus_top = keep.tile([P, 4], F32, name="minus_top")
+        nc.vector.tensor_reduce(minus_top[:], s, AX.X, ALU.max, negate=True)
+        e = keep.tile([P, 4, D], F32, name="e")
+        den = keep.tile([P, 4], F32, name="den")
+        for c in range(4):
+            nc.scalar.activation(
+                e[:, c, :], s[:, c, :], ACT.Exp, bias=minus_top[:, c : c + 1], accum_out=den[:, c : c + 1]
+            )
+        inv = keep.tile([P, 4], F32, name="inv")
+        nc.vector.reciprocal(inv[:], den[:])
+        a = keep.tile([P, 4, D], F32, name="a")
+        nc.vector.tensor_tensor(a[:], e[:], inv[:].unsqueeze(2).to_broadcast([P, 4, D]), ALU.mult)
 
         def project(b, w_mx, k, c0, c1, engine_copy):
             codes, scales = w_mx
@@ -111,21 +113,18 @@ def tile_picked_wgatv_relu_l_kernel(
         def spread(d, k):
             ps = bank(k, [P, 4, P], "spread%d" % d)
             for c in range(4):
-                nc.tensor.transpose(ps[:, c, :], shifted[:, c, d : d + 1].to_broadcast([P, P]), ident[:])
+                nc.tensor.transpose(ps[:, c, :], a[:, c, d : d + 1].to_broadcast([P, P]), ident[:])
             wide = keep.tile([P, T], F32, name="wide%d" % d)
-            nc.scalar.activation(wide[:], ps[:].rearrange("p c n -> p (c n)"), ACT.Exp)
+            nc.scalar.copy(wide[:], ps[:].rearrange("p c n -> p (c n)"))
             return wide
 
-        w0 = quantise(0, nc.vector.tensor_copy)
-        project(0, w0, 1, 0, T // 2, nc.vector.tensor_copy)
-        project(0, w0, 2, T // 2, T, nc.scalar.copy)
+        for c in range(2):
+            project(0, w0, 1 + c, c * T // 2, (c + 1) * T // 2, nc.scalar.copy)
+        w1q = quantise(1, (nc.vector.tensor_copy,))
         wide = {}
-        wide[1] = spread(1, 1)
-        w1q = quantise(1, nc.scalar.copy)
-        wide[2] = spread(2, 2)
-        wide[3] = spread(3, 1)
-        project(1, w1q, 3, 0, T, nc.scalar.copy)
-        wide[0] = spread(0, 2)
+        for k, d in enumerate((1, 2, 3, 0)):
+            wide[d] = spread(d, 1 + k)
+        project(1, w1q, 1, 0, T, nc.scalar.copy)
 
         def gather(b, d, h, c0, c1):
             nc.vector.tensor_tensor(
@@ -140,41 +139,21 @@ def tile_picked_wgatv_relu_l_kernel(
                     start=(d == first and c == 0), stop=(d == D - 1 and c == n - 1),
                 )
 
-        def finish(b, acc, k, c0, c1, on_vector):
-            n = (c1 - c0) // P
-            turned = keep.tile([P, n, P], F32, name="turned%d_%d" % (b, c0))
-            for c in range(n):
-                scale = inv[:, c0 // P + c : c0 // P + c + 1]
-                if on_vector:
-                    nc.vector.tensor_scalar(turned[:, c, :], acc[:, c, :], scale, 0.0, ALU.mult, ALU.max)
-                else:
-                    nc.scalar.activation(turned[:, c, :], acc[:, c, :], ACT.Relu, scale=scale)
-            back = bank(k, [P, n, P], "back%d_%d" % (b, c0))
-            for c in range(n):
-                nc.tensor.transpose(back[:, c, :], turned[:, c, :], ident[:])
-            res = keep.tile([P, n, P], F32, name="res%d_%d" % (b, c0))
-            if on_vector:
-                nc.vector.tensor_copy(res[:], back[:])
-            else:
-                nc.scalar.copy(res[:], back[:])
-            nc.sync.dma_start(out[b * P : (b + 1) * P, c0:c1], res[:].rearrange("p c n -> p (c n)"))
-
         g = keep.tile([P, T], F32, name="g0")
         nc.vector.tensor_copy(g[:], y[0][:].indirect(lists[0][:]))
-        g_ps = bank(4, [P, 4, P], "g_ps")
+        g_ps = bank(2, [P, 4, P], "g_ps")
         for c in range(4):
             nc.tensor.transpose(g_ps[:, c, :], g[:, c * P : (c + 1) * P], ident[:])
         g_turned = keep.tile([P, 4, P], F32, name="g_turned")
         for c in range(4):
-            nc.scalar.activation(g_turned[:, c, :], g_ps[:, c, :], ACT.Copy, scale=a0[:, c : c + 1])
-        acc0 = bank(5, [P, 4, P], "sum0")
+            nc.scalar.activation(g_turned[:, c, :], g_ps[:, c, :], ACT.Copy, scale=a[:, c, 0:1])
+        acc0 = bank(3, [P, 4, P], "sum0")
         for d in range(1, D):
             h = keep.tile([P, T], F32, name="h0_%d" % d)
             gather(0, d, h, 0, T)
             add_turned(h, acc0, d, 0, T, 1)
-        turned0 = keep.tile([P, 4, P], F32, name="turned0")
-        for c in range(4):
-            nc.scalar.activation(turned0[:, c, :], acc0[:, c, :], ACT.Copy, scale=inv[:, c : c + 1])
+        turned0 = keep.tile([P, 4, P], F32, name="turned0", tag="late")
+        nc.scalar.copy(turned0[:], acc0[:])
         back0 = bank(0, [P, 4, P], "back0")
         for j, src in enumerate((g_turned, turned0)):
             for c in range(4):
@@ -184,18 +163,25 @@ def tile_picked_wgatv_relu_l_kernel(
                 )
         res0 = keep.tile([P, T], F32, name="res0")
         nc.scalar.activation(res0[:], back0[:].rearrange("p c n -> p (c n)"), ACT.Relu)
-        nc.sync.dma_start(out[0:P, :], res0[:])
+        nc.scalar.dma_start(out[0:P, :], res0[:])
 
-        pieces = ((0, 256, 4, 1), (256, 384, 6, 2), (384, 512, 7, 3))
-        accs = [bank(k, [P, (c1 - c0) // P, P], "sum1_%d" % c0) for c0, c1, k, kb in pieces]
-        for d in range(D - 1):
-            h = keep.tile([P, T], F32, name="h1_%d" % d)
-            gather(1, d, h, 0, T)
-            for acc, (c0, c1, k, kb) in zip(accs, pieces):
-                add_turned(h, acc, d, c0, c1)
-        h = keep.tile([P, T], F32, name="h1_3")
-        for acc, (c0, c1, k, kb) in zip(accs, pieces):
-            gather(1, D - 1, h, c0, c1)
-            add_turned(h, acc, D - 1, c0, c1)
-        for acc, (c0, c1, k, kb) in zip(accs, pieces):
-            finish(1, acc, kb, c0, c1, c1 == T)
+        h = [keep.tile([P, T], F32, name="h1_%d" % d) for d in range(D)]
+        for d in range(3):
+            gather(1, d, h[d], 0, T)
+        u01 = keep.tile([P, T], F32, name="u01")
+        nc.vector.tensor_tensor(u01[:], h[0][:], h[1][:], ALU.add)
+        gather(1, 3, h[3], 0, 256)
+        u012 = keep.tile([P, T], F32, name="u012")
+        nc.vector.tensor_tensor(u012[:], u01[:], h[2][:], ALU.add)
+        gather(1, 3, h[3], 256, T)
+        for c0, c1 in ((0, 256), (256, T)):
+            total = keep.tile([P, c1 - c0], F32, name="total%d" % c0)
+            nc.vector.tensor_tensor(total[:], u012[:, c0:c1], h[3][:, c0:c1], ALU.add)
+            if c0 == 0:
+                res = keep.tile([P, c1 - c0], F32, name="res1_a", tag="late")
+                nc.scalar.activation(res[:], total[:], ACT.Relu)
+                nc.scalar.dma_start(out[P : 2 * P, c0:c1], res[:])
+            else:
+                res = keep.tile([P, c1 - c0], F32, name="res1_b")
+                nc.vector.tensor_scalar_max(res[:], total[:], 0.0)
+                nc.sync.dma_start(out[P : 2 * P, c0:c1], res[:])

@@ -121,22 +121,22 @@ def tile_picked_wgatv_relu_l_kernel(
         for c in range(2):
             project(0, w0, 1 + c, c * T // 2, (c + 1) * T // 2, nc.scalar.copy)
         w1q = quantise(1, (nc.vector.tensor_copy,))
+        project(1, w1q, 5, 0, T, nc.scalar.copy)
         wide = {}
         for k, d in enumerate((1, 2, 3, 0)):
             wide[d] = spread(d, 1 + k)
-        project(1, w1q, 1, 0, T, nc.scalar.copy)
 
         def gather(b, d, h, c0, c1):
             nc.vector.tensor_tensor(
                 h[:, c0:c1], y[b][:].indirect(lists[d][:, c0 // 16 : c1 // 16]), wide[d][:, c0:c1], ALU.mult
             )
 
-        def add_turned(h, acc, d, c0, c1, first=0):
+        def add_turned(h, acc, d, c0, c1, first, last):
             n = (c1 - c0) // P
             for c in range(n):
                 nc.tensor.matmul(
                     acc[:, c, :], lhsT=h[:, c0 + c * P : c0 + (c + 1) * P], rhs=ident[:], is_transpose=True,
-                    start=(d == first and c == 0), stop=(d == D - 1 and c == n - 1),
+                    start=(d == first and c == 0), stop=(d == last and c == n - 1),
                 )
 
         g = keep.tile([P, T], F32, name="g0")
@@ -151,8 +151,8 @@ def tile_picked_wgatv_relu_l_kernel(
         for d in range(1, D):
             h = keep.tile([P, T], F32, name="h0_%d" % d)
             gather(0, d, h, 0, T)
-            add_turned(h, acc0, d, 0, T, 1)
-        turned0 = keep.tile([P, 4, P], F32, name="turned0", tag="late")
+            add_turned(h, acc0, d, 0, T, 1, 3)
+        turned0 = keep.tile([P, 4, P], F32, name="turned0")
         nc.scalar.copy(turned0[:], acc0[:])
         back0 = bank(0, [P, 4, P], "back0")
         for j, src in enumerate((g_turned, turned0)):
@@ -165,23 +165,36 @@ def tile_picked_wgatv_relu_l_kernel(
         nc.scalar.activation(res0[:], back0[:].rearrange("p c n -> p (c n)"), ACT.Relu)
         nc.scalar.dma_start(out[0:P, :], res0[:])
 
+        half = T // 2
         h = [keep.tile([P, T], F32, name="h1_%d" % d) for d in range(D)]
-        for d in range(3):
-            gather(1, d, h[d], 0, T)
-        u01 = keep.tile([P, T], F32, name="u01")
-        nc.vector.tensor_tensor(u01[:], h[0][:], h[1][:], ALU.add)
-        gather(1, 3, h[3], 0, 256)
-        u012 = keep.tile([P, T], F32, name="u012")
-        nc.vector.tensor_tensor(u012[:], u01[:], h[2][:], ALU.add)
-        gather(1, 3, h[3], 256, T)
-        for c0, c1 in ((0, 256), (256, T)):
-            total = keep.tile([P, c1 - c0], F32, name="total%d" % c0)
-            nc.vector.tensor_tensor(total[:], u012[:, c0:c1], h[3][:, c0:c1], ALU.add)
-            if c0 == 0:
-                res = keep.tile([P, c1 - c0], F32, name="res1_a", tag="late")
-                nc.scalar.activation(res[:], total[:], ACT.Relu)
-                nc.scalar.dma_start(out[P : 2 * P, c0:c1], res[:])
-            else:
-                res = keep.tile([P, c1 - c0], F32, name="res1_b")
-                nc.vector.tensor_scalar_max(res[:], total[:], 0.0)
-                nc.sync.dma_start(out[P : 2 * P, c0:c1], res[:])
+        acc1 = bank(3, [P, 2, P], "sum1")
+        for d in range(D):
+            gather(1, d, h[d], 0, T if d < 2 else half)
+            add_turned(h[d], acc1, d, 0, half, 0, 3)
+        turned1 = keep.tile([P, 2, P], F32, name="turned1")
+        nc.scalar.activation(turned1[:], acc1[:], ACT.Relu)
+        back1 = bank(6, [P, 2, P], "back1")
+        for c in range(2):
+            nc.tensor.transpose(back1[:, c, :], turned1[:, c, :], ident[:])
+        res1 = keep.tile([P, half], F32, name="res1")
+        nc.scalar.copy(res1[:], back1[:].rearrange("p c n -> p (c n)"))
+        nc.scalar.dma_start(out[P : 2 * P, 0:half], res1[:])
+
+        gather(1, 2, h[2], half, T)
+        u01 = keep.tile([P, half], F32, name="u01")
+        nc.vector.tensor_tensor(u01[:], h[0][:, half:], h[1][:, half:], ALU.add)
+        gather(1, 3, h[3], half, half + P)
+        u012 = keep.tile([P, half], F32, name="u012")
+        nc.vector.tensor_tensor(u012[:], u01[:], h[2][:, half:], ALU.add)
+        gather(1, 3, h[3], half + P, T)
+        totals = []
+        for c in range(2):
+            total = keep.tile([P, P], F32, name="total%d" % c)
+            nc.vector.tensor_tensor(
+                total[:], u012[:, c * P : (c + 1) * P], h[3][:, half + c * P : half + (c + 1) * P], ALU.add
+            )
+            totals.append(total)
+        for c in range(2):
+            res = keep.tile([P, P], F32, name="res2_%d" % c)
+            nc.vector.tensor_scalar_max(res[:], totals[c][:], 0.0)
+            nc.sync.dma_start(out[P : 2 * P, half + c * P : half + (c + 1) * P], res[:])

from contextlib import ExitStack

import concourse.mybir as mybir

K, T, D, N = 512, 512, 4, 256
P = 128
PACK = 4
PAD = 192

FLOPS = 2 * K * N * T
BYTES = K * T // 2 + K * T // 32 + 4 * K * N + 4 * D * T + 2 * D * P * (T // 16) + 4 * N * T

F32 = mybir.dt.float32
BF16 = mybir.dt.bfloat16
I32 = mybir.dt.int32
U32 = mybir.dt.uint32
U16 = mybir.dt.uint16
U8 = mybir.dt.uint8
FP8X4 = mybir.dt.float8_e4m3fn_x4
FP4X4 = mybir.dt.float4_e2m1fn_x4
ALU = mybir.AluOpType
ACT = mybir.ActivationFunctionType
AX = mybir.AxisListType


def tile_picked_wgatv_relu_l_kernel(
    tc, x_words, x_scales, w1, score, pos1, pos2, pos3, pos4, out
):
    nc = tc.nc
    with ExitStack() as ctx:
        keep = ctx.enter_context(tc.tile_pool(name="keep", bufs=1))
        psum = ctx.enter_context(tc.psum_pool(name="psum", bufs=1))

        def bank(k, shape, name):
            return psum.tile(shape, F32, tag="bank%d" % k, name=name)

        w_raw = [keep.tile([P, PACK, P], F32, name="w_raw%d" % b) for b in range(2)]
        w_rows = w1.rearrange("(p j) n -> p j n", j=PACK)
        nc.sync.dma_start(w_raw[0][:], w_rows[:, :, 0:P])
        s_rows = keep.tile([P, P], F32, name="s_rows")
        nc.sync.dma_start(s_rows[:], score.rearrange("d r (c q) -> (r c) d q", q=P)[0:32])
        xw = keep.tile([P, 2 * T], U8, name="xw", align_bytes=64)
        nc.sync.dma_start(xw[:].bitcast(I32), x_words[0].bitcast(I32))
        nc.sync.dma_start(w_raw[1][:], w_rows[:, :, P : 2 * P])
        xs = keep.tile([P, T], U8, name="xs", align_bytes=64)
        for q in range(4):
            nc.scalar.dma_start(
                xs[32 * q : 32 * (q + 1), :].bitcast(I32),
                x_scales[0, 4 * q : 4 * (q + 1), :].bitcast(I32).partition_broadcast(8),
            )
        lists = []
        for d, pos in enumerate((pos1, pos2, pos3, pos4)):
            offsets = keep.tile([P, T // 16], U16, name="offsets%d" % d)
            nc.sync.dma_start(offsets[:], pos)
            lists.append(offsets)

        ident = keep.tile([P, P], F32, name="ident")
        ones = keep.tile([P, 32], F32, name="ones")
        nc.vector.memset(ones[:], 1.0)
        nc.gpsimd.memset(ident[:], 0.0)
        column = keep.tile([P, 32], F32, name="column", align_bytes=64)
        nc.vector.tensor_tensor_scan(column[:], ones[:], ones[:], 0.0, ALU.mult, ALU.add)
        row = keep.tile([P, 32], F32, name="row", align_bytes=64)
        nc.vector.transpose(row[:], column[:])
        for q in range(4):
            part = slice(32 * q, 32 * (q + 1))
            nc.vector.tensor_tensor(ident[part, part], column[part, :], row[part, :], ALU.is_equal)
        y = []
        for b in range(2):
            yb = keep.tile([P, T + PAD], F32, name="y%d" % b)
            nc.gpsimd.memset(yb[:, T:], 0.0)
            y.append(yb)

        def quantise(b, copies):
            grouped = keep.tile([P, P, PACK], BF16, name="grouped%d" % b, align_bytes=64)
            n = P // len(copies)
            for j, engine_copy in enumerate(copies):
                engine_copy(
                    grouped[:, j * n : (j + 1) * n, :].rearrange("p (c i) t -> p c t i", i=4),
                    w_raw[b][:, :, j * n : (j + 1) * n].rearrange("p t (c i) -> p c t i", i=4),
                )
            codes = keep.tile([P, P], U32, name="codes%d" % b, align_bytes=64)
            scales = keep.tile([P, P], U8, name="scales%d" % b, align_bytes=64)
            nc.vector.quantize_mx(codes[:].bitcast(FP8X4), scales[:], grouped[:].rearrange("p m t -> p (m t)"))
            return codes, scales

        w0 = quantise(0, (nc.vector.tensor_copy,))
        s_ps = bank(0, [P, P], "s_ps")
        nc.tensor.transpose(s_ps[:], s_rows[:], ident[:])
        s = s_ps[:, 0:16].rearrange("q (c d) -> q c d", d=D)
        minus_top = keep.tile([P, 4], F32, name="minus_top")
        nc.vector.tensor_reduce(minus_top[:], s, AX.X, ALU.max, negate=True)
        e = keep.tile([P, 4, D], F32, name="e")
        den = keep.tile([P, 4], F32, name="den")
        for c in range(4):
            nc.scalar.activation(
                e[:, c, :], s[:, c, :], ACT.Exp, bias=minus_top[:, c : c + 1], accum_out=den[:, c : c + 1]
            )
        inv = keep.tile([P, 4], F32, name="inv")
        nc.vector.reciprocal(inv[:], den[:])
        a = keep.tile([P, 4, D], F32, name="a")
        nc.vector.tensor_tensor(a[:], e[:], inv[:].unsqueeze(2).to_broadcast([P, 4, D]), ALU.mult)

        def project(b, w_mx, k, c0, c1, engine_copy):
            codes, scales = w_mx
            acc = bank(k, [P, c1 - c0], "acc%d_%d" % (b, c0))
            nc.tensor.matmul_mx(
                acc[:], lhsT=codes[:].bitcast(FP8X4), lhsT_scale=scales[:],
                rhs=xw[:, 2 * c0 : 2 * c1].bitcast(FP4X4), rhs_scale=xs[:, c0:c1], start=True, stop=True,
            )
            engine_copy(y[b][:, c0:c1], acc[:])

        def spread(d, k):
            ps = bank(k, [P, 4, P], "spread%d" % d)
            for c in range(4):
                nc.tensor.transpose(ps[:, c, :], a[:, c, d : d + 1].to_broadcast([P, P]), ident[:])
            wide = keep.tile([P, T], F32, name="wide%d" % d)
            nc.scalar.copy(wide[:], ps[:].rearrange("p c n -> p (c n)"))
            return wide

        for c in range(2):
            project(0, w0, 1 + c, c * T // 2, (c + 1) * T // 2, nc.scalar.copy)
        w1q = quantise(1, (nc.vector.tensor_copy,))
        project(1, w1q, 5, 0, T, nc.scalar.copy)
        wide = {}
        for k, d in enumerate((1, 2, 3, 0)):
            wide[d] = spread(d, 1 + k)

        def gather(b, d, h, c0, c1):
            nc.vector.tensor_tensor(
                h[:, c0:c1], y[b][:].indirect(lists[d][:, c0 // 16 : c1 // 16]), wide[d][:, c0:c1], ALU.mult
            )

        def add_turned(h, acc, d, c0, c1, first, last):
            n = (c1 - c0) // P
            for c in range(n):
                nc.tensor.matmul(
                    acc[:, c, :], lhsT=h[:, c0 + c * P : c0 + (c + 1) * P], rhs=ident[:], is_transpose=True,
                    start=(d == first and c == 0), stop=(d == last and c == n - 1),
                )

        g = keep.tile([P, T], F32, name="g0")
        nc.vector.tensor_copy(g[:], y[0][:].indirect(lists[0][:]))
        g_ps = bank(2, [P, 4, P], "g_ps")
        for c in range(4):
            nc.tensor.transpose(g_ps[:, c, :], g[:, c * P : (c + 1) * P], ident[:])
        g_turned = keep.tile([P, 4, P], F32, name="g_turned")
        for c in range(4):
            nc.scalar.activation(g_turned[:, c, :], g_ps[:, c, :], ACT.Copy, scale=a[:, c, 0:1])
        acc0 = bank(3, [P, 4, P], "sum0")
        for d in range(1, D):
            h = keep.tile([P, T], F32, name="h0_%d" % d)
            gather(0, d, h, 0, T)
            add_turned(h, acc0, d, 0, T, 1, 3)
        turned0 = keep.tile([P, 4, P], F32, name="turned0")
        nc.scalar.copy(turned0[:], acc0[:])
        back0 = bank(0, [P, 4, P], "back0")
        for j, src in enumerate((g_turned, turned0)):
            for c in range(4):
                nc.tensor.matmul(
                    back0[:, c, :], lhsT=src[:, c, :], rhs=ident[:], is_transpose=True,
                    start=(j == 0 and c == 0), stop=(j == 1 and c == 3),
                )
        res0 = keep.tile([P, T], F32, name="res0")
        nc.scalar.activation(res0[:], back0[:].rearrange("p c n -> p (c n)"), ACT.Relu)
        nc.scalar.dma_start(out[0:P, :], res0[:])

        half = T // 2
        h = [keep.tile([P, T], F32, name="h1_%d" % d) for d in range(D)]
        acc1 = bank(3, [P, 2, P], "sum1")
        for d in range(D):
            gather(1, d, h[d], 0, T if d < 2 else half)
            add_turned(h[d], acc1, d, 0, half, 0, 3)
        turned1 = keep.tile([P, 2, P], F32, name="turned1")
        nc.scalar.activation(turned1[:], acc1[:], ACT.Relu)
        back1 = bank(6, [P, 2, P], "back1")
        for c in range(2):
            nc.tensor.transpose(back1[:, c, :], turned1[:, c, :], ident[:])
        res1 = keep.tile([P, half], F32, name="res1")
        nc.scalar.copy(res1[:], back1[:].rearrange("p c n -> p (c n)"))
        nc.scalar.dma_start(out[P : 2 * P, 0:half], res1[:])

        gather(1, 2, h[2], half, T)
        u01 = keep.tile([P, half], F32, name="u01")
        nc.vector.tensor_tensor(u01[:], h[0][:, half:], h[1][:, half:], ALU.add)
        gather(1, 3, h[3], half, half + P)
        u012 = keep.tile([P, half], F32, name="u012")
        nc.vector.tensor_tensor(u012[:], u01[:], h[2][:, half:], ALU.add)
        gather(1, 3, h[3], half + P, T)
        totals = []
        for c in range(2):
            total = keep.tile([P, P], F32, name="total%d" % c)
            nc.vector.tensor_tensor(
                total[:], u012[:, c * P : (c + 1) * P], h[3][:, half + c * P : half + (c + 1) * P], ALU.add
            )
            totals.append(total)
        for c in range(2):
            res = keep.tile([P, P], F32, name="res2_%d" % c)
            nc.vector.tensor_scalar_max(res[:], totals[c][:], 0.0)
            nc.sync.dma_start(out[P : 2 * P, half + c * P : half + (c + 1) * P], res[:])
